import numpy as np
import ml_dtypes

BF16 = ml_dtypes.bfloat16


def bf(x):
    return np.asarray(x, np.float32).astype(BF16)


def f32(x):
    return np.asarray(x, np.float32)


def f64(x):
    return np.asarray(x).astype(np.float64)


def striped(idx):
    return np.tile(idx.reshape(-1, 16).T, (8, 1))


S, K, M, N, D, V = 1024, 256, 128, 256, 4, 64


def gelu_tanh(v):
    return 0.5 * v * (1.0 + np.tanh(np.sqrt(2.0 / np.pi) * (v + 0.044715 * v**3)))


def setup_inputs():
    return {"table": bf(np.random.standard_normal((K, S))), "w": bf(np.random.standard_normal((K, M)) / np.sqrt(K)), "b": f32(0.5 * np.random.standard_normal((M, 1))), "offs": striped(np.random.permutation(np.tile(np.arange(S), 2))[:N])}


def reference(table, w, b, offs):
    idx = offs[:16].T.reshape(-1)
    x = f64(table)[:, idx]
    y = f64(w).T @ x
    z = gelu_tanh(y + f64(b))
    return z.reshape(M, V, D).max(axis=2)

@@ -1,0 +1,48 @@
+import concourse.mybir as mybir
+
+BF16, F32, U16 = mybir.dt.bfloat16, mybir.dt.float32, mybir.dt.uint16
+
+P = 128
+K, S, M, N = 256, 1024, 128, 256
+K_BLOCKS = K // P
+NEIGHBOURS = 4
+FLOPS = 2 * K * M * N
+
+
+def tile_gather_matmul_kernel(tc, table, w, b, offs, out):
+    nc = tc.nc
+    with (
+        tc.tile_pool(name="held", bufs=1) as held,
+        tc.psum_pool(name="psum", bufs=1) as psum,
+    ):
+        offsets = held.tile([P, N // 16], U16, name="offsets")
+        nc.sync.dma_start(offsets[:], offs)
+        weights = held.tile([P, K_BLOCKS, M], BF16, name="weights")
+        nc.scalar.dma_start(weights[:], w.rearrange("(a p) m -> p a m", p=P))
+        windows = [held.tile([P, S], BF16, name="window%d" % a) for a in range(K_BLOCKS)]
+        nc.sync.dma_start(windows[0][:], table[0:P, :])
+        nc.scalar.dma_start(windows[1][:], table[P : 2 * P, :])
+        bias = held.tile([P, 1], F32, name="bias")
+        nc.sync.dma_start(bias[:], b)
+
+        y = psum.tile([P, N], F32, name="y")
+        for a in range(K_BLOCKS):
+            nc.tensor.matmul(
+                y[:],
+                weights[:, a, :],
+                windows[a][:].indirect(offsets[:]),
+                start=(a == 0),
+                stop=(a == K_BLOCKS - 1),
+            )
+
+        z = held.tile([P, N], F32, name="z")
+        nc.scalar.activation(z[:], y[:], mybir.ActivationFunctionType.Gelu_apprx_tanh, bias=bias[:, 0:1])
+
+        pooled = held.tile([P, N // NEIGHBOURS], F32, name="pooled")
+        nc.vector.tensor_reduce(
+            pooled[:],
+            z[:].rearrange("p (v t) -> p v t", t=NEIGHBOURS),
+            axis=mybir.AxisListType.X,
+            op=mybir.AluOpType.max,
+        )
+        nc.sync.dma_start(out, pooled[:])

@@ -25,6 +25,11 @@ def tile_gather_matmul_kernel(tc, table, w, b, offs, out):
         bias = held.tile([P, 1], F32, name="bias")
         nc.sync.dma_start(bias[:], b)
 
+        warm_in = held.tile([P, 1], F32, name="warm_in")
+        warm_out = held.tile([P, 1], F32, name="warm_out")
+        nc.vector.memset(warm_in[:], 0.0)
+        nc.scalar.activation(warm_out[:], warm_in[:], mybir.ActivationFunctionType.Gelu_apprx_tanh)
+
         y = psum.tile([P, N], F32, name="y")
         for a in range(K_BLOCKS):
             nc.tensor.matmul(

@@ -6,6 +6,8 @@ P = 128
 K, S, M, N = 256, 1024, 128, 256
 K_BLOCKS = K // P
 NEIGHBOURS = 4
+PIECES = 2
+PIECE = N // PIECES
 FLOPS = 2 * K * M * N
 
 
@@ -21,33 +23,35 @@ def tile_gather_matmul_kernel(tc, table, w, b, offs, out):
         nc.scalar.dma_start(weights[:], w.rearrange("(a p) m -> p a m", p=P))
         windows = [held.tile([P, S], BF16, name="window%d" % a) for a in range(K_BLOCKS)]
         nc.sync.dma_start(windows[0][:], table[0:P, :])
-        nc.scalar.dma_start(windows[1][:], table[P : 2 * P, :])
+        nc.sync.dma_start(windows[1][:], table[P : 2 * P, :])
         bias = held.tile([P, 1], F32, name="bias")
-        nc.sync.dma_start(bias[:], b)
+        nc.scalar.dma_start(bias[:], b)
 
         warm_in = held.tile([P, 1], F32, name="warm_in")
         warm_out = held.tile([P, 1], F32, name="warm_out")
         nc.vector.memset(warm_in[:], 0.0)
         nc.scalar.activation(warm_out[:], warm_in[:], mybir.ActivationFunctionType.Gelu_apprx_tanh)
 
-        y = psum.tile([P, N], F32, name="y")
+        y = [psum.tile([P, PIECE], F32, name="y%d" % i) for i in range(PIECES)]
         for a in range(K_BLOCKS):
-            nc.tensor.matmul(
-                y[:],
-                weights[:, a, :],
-                windows[a][:].indirect(offsets[:]),
-                start=(a == 0),
-                stop=(a == K_BLOCKS - 1),
-            )
+            for i in range(PIECES):
+                nc.tensor.matmul(
+                    y[i][:],
+                    weights[:, a, :],
+                    windows[a][:].indirect(offsets[:, i * (PIECE // 16) : (i + 1) * (PIECE // 16)]),
+                    start=(a == 0),
+                    stop=(a == K_BLOCKS - 1),
+                )
 
         z = held.tile([P, N], F32, name="z")
-        nc.scalar.activation(z[:], y[:], mybir.ActivationFunctionType.Gelu_apprx_tanh, bias=bias[:, 0:1])
-
         pooled = held.tile([P, N // NEIGHBOURS], F32, name="pooled")
-        nc.vector.tensor_reduce(
-            pooled[:],
-            z[:].rearrange("p (v t) -> p v t", t=NEIGHBOURS),
-            axis=mybir.AxisListType.X,
-            op=mybir.AluOpType.max,
-        )
+        for i in range(PIECES):
+            z_piece = z[:, i * PIECE : (i + 1) * PIECE]
+            nc.scalar.activation(z_piece, y[i][:], mybir.ActivationFunctionType.Gelu_apprx_tanh, bias=bias[:, 0:1])
+            nc.vector.tensor_reduce(
+                pooled[:, i * (PIECE // NEIGHBOURS) : (i + 1) * (PIECE // NEIGHBOURS)],
+                z_piece.rearrange("p (v t) -> p v t", t=NEIGHBOURS),
+                axis=mybir.AxisListType.X,
+                op=mybir.AluOpType.max,
+            )
         nc.sync.dma_start(out, pooled[:])

@@ -8,6 +8,7 @@ K_BLOCKS = K // P
 NEIGHBOURS = 4
 PIECES = 2
 PIECE = N // PIECES
+WARM_MATMULS = 16
 FLOPS = 2 * K * M * N
 
 
@@ -27,10 +28,13 @@ def tile_gather_matmul_kernel(tc, table, w, b, offs, out):
         bias = held.tile([P, 1], F32, name="bias")
         nc.scalar.dma_start(bias[:], b)
 
-        warm_in = held.tile([P, 1], F32, name="warm_in")
-        warm_out = held.tile([P, 1], F32, name="warm_out")
-        nc.vector.memset(warm_in[:], 0.0)
-        nc.scalar.activation(warm_out[:], warm_in[:], mybir.ActivationFunctionType.Gelu_apprx_tanh)
+        zeros = held.tile([P, P], BF16, name="zeros")
+        nc.vector.memset(zeros[:], 0.0)
+        unused_product = psum.tile([P, P], F32, name="unused_product")
+        for r in range(WARM_MATMULS):
+            nc.tensor.matmul(unused_product[:], zeros[:], zeros[:], start=True, stop=True)
+        unused_gelu = held.tile([P, 1], F32, name="unused_gelu")
+        nc.scalar.activation(unused_gelu[:], zeros[:, 0:1], mybir.ActivationFunctionType.Gelu_apprx_tanh)
 
         y = [psum.tile([P, PIECE], F32, name="y%d" % i) for i in range(PIECES)]
         for a in range(K_BLOCKS):

@@ -8,7 +8,6 @@ K_BLOCKS = K // P
 NEIGHBOURS = 4
 PIECES = 2
 PIECE = N // PIECES
-WARM_MATMULS = 16
 FLOPS = 2 * K * M * N
 
 
@@ -23,18 +22,16 @@ def tile_gather_matmul_kernel(tc, table, w, b, offs, out):
         weights = held.tile([P, K_BLOCKS, M], BF16, name="weights")
         nc.scalar.dma_start(weights[:], w.rearrange("(a p) m -> p a m", p=P))
         windows = [held.tile([P, S], BF16, name="window%d" % a) for a in range(K_BLOCKS)]
-        nc.sync.dma_start(windows[0][:], table[0:P, :])
-        nc.sync.dma_start(windows[1][:], table[P : 2 * P, :])
+        for a in range(K_BLOCKS):
+            nc.sync.dma_start(windows[a][:, 0 : S // 2], table[a * P : (a + 1) * P, 0 : S // 2])
+            nc.scalar.dma_start(windows[a][:, S // 2 : S], table[a * P : (a + 1) * P, S // 2 : S])
         bias = held.tile([P, 1], F32, name="bias")
         nc.scalar.dma_start(bias[:], b)
 
-        zeros = held.tile([P, P], BF16, name="zeros")
-        nc.vector.memset(zeros[:], 0.0)
-        unused_product = psum.tile([P, P], F32, name="unused_product")
-        for r in range(WARM_MATMULS):
-            nc.tensor.matmul(unused_product[:], zeros[:], zeros[:], start=True, stop=True)
-        unused_gelu = held.tile([P, 1], F32, name="unused_gelu")
-        nc.scalar.activation(unused_gelu[:], zeros[:, 0:1], mybir.ActivationFunctionType.Gelu_apprx_tanh)
+        warm_in = held.tile([P, 1], F32, name="warm_in")
+        warm_out = held.tile([P, 1], F32, name="warm_out")
+        nc.vector.memset(warm_in[:], 0.0)
+        nc.scalar.activation(warm_out[:], warm_in[:], mybir.ActivationFunctionType.Gelu_apprx_tanh)
 
         y = [psum.tile([P, PIECE], F32, name="y%d" % i) for i in range(PIECES)]
         for a in range(K_BLOCKS):

@@ -20,13 +20,12 @@ def tile_gather_matmul_kernel(tc, table, w, b, offs, out):
         offsets = held.tile([P, N // 16], U16, name="offsets")
         nc.sync.dma_start(offsets[:], offs)
         weights = held.tile([P, K_BLOCKS, M], BF16, name="weights")
-        nc.scalar.dma_start(weights[:], w.rearrange("(a p) m -> p a m", p=P))
+        nc.sync.dma_start(weights[:], w.rearrange("(a p) m -> p a m", p=P))
+        bias = held.tile([P, 1], F32, name="bias")
+        nc.sync.dma_start(bias[:], b)
         windows = [held.tile([P, S], BF16, name="window%d" % a) for a in range(K_BLOCKS)]
         for a in range(K_BLOCKS):
-            nc.sync.dma_start(windows[a][:, 0 : S // 2], table[a * P : (a + 1) * P, 0 : S // 2])
-            nc.scalar.dma_start(windows[a][:, S // 2 : S], table[a * P : (a + 1) * P, S // 2 : S])
-        bias = held.tile([P, 1], F32, name="bias")
-        nc.scalar.dma_start(bias[:], b)
+            nc.scalar.dma_start(windows[a][:], table[a * P : (a + 1) * P, :])
 
         warm_in = held.tile([P, 1], F32, name="warm_in")
         warm_out = held.tile([P, 1], F32, name="warm_out")

@@ -20,12 +20,13 @@ def tile_gather_matmul_kernel(tc, table, w, b, offs, out):
         offsets = held.tile([P, N // 16], U16, name="offsets")
         nc.sync.dma_start(offsets[:], offs)
         weights = held.tile([P, K_BLOCKS, M], BF16, name="weights")
-        nc.sync.dma_start(weights[:], w.rearrange("(a p) m -> p a m", p=P))
+        nc.sync.dma_start(weights[:], w.rearrange("(p a) m -> p a m", a=K_BLOCKS))
         bias = held.tile([P, 1], F32, name="bias")
         nc.sync.dma_start(bias[:], b)
         windows = [held.tile([P, S], BF16, name="window%d" % a) for a in range(K_BLOCKS)]
+        table_rows = table.rearrange("(p a) s -> p a s", a=K_BLOCKS)
         for a in range(K_BLOCKS):
-            nc.scalar.dma_start(windows[a][:], table[a * P : (a + 1) * P, :])
+            nc.scalar.dma_start(windows[a][:], table_rows[:, a, :])
 
         warm_in = held.tile([P, 1], F32, name="warm_in")
         warm_out = held.tile([P, 1], F32, name="warm_out")

@@ -8,6 +8,7 @@ K_BLOCKS = K // P
 NEIGHBOURS = 4
 PIECES = 2
 PIECE = N // PIECES
+ROW_ALIGN = 256
 FLOPS = 2 * K * M * N
 
 
@@ -17,13 +18,13 @@ def tile_gather_matmul_kernel(tc, table, w, b, offs, out):
         tc.tile_pool(name="held", bufs=1) as held,
         tc.psum_pool(name="psum", bufs=1) as psum,
     ):
-        offsets = held.tile([P, N // 16], U16, name="offsets")
+        offsets = held.tile([P, N // 16], U16, name="offsets", align_bytes=ROW_ALIGN)
         nc.sync.dma_start(offsets[:], offs)
-        weights = held.tile([P, K_BLOCKS, M], BF16, name="weights")
+        weights = held.tile([P, K_BLOCKS, M], BF16, name="weights", align_bytes=ROW_ALIGN)
         nc.sync.dma_start(weights[:], w.rearrange("(p a) m -> p a m", a=K_BLOCKS))
-        bias = held.tile([P, 1], F32, name="bias")
+        bias = held.tile([P, 1], F32, name="bias", align_bytes=ROW_ALIGN)
         nc.sync.dma_start(bias[:], b)
-        windows = [held.tile([P, S], BF16, name="window%d" % a) for a in range(K_BLOCKS)]
+        windows = [held.tile([P, S], BF16, name="window%d" % a, align_bytes=ROW_ALIGN) for a in range(K_BLOCKS)]
         table_rows = table.rearrange("(p a) s -> p a s", a=K_BLOCKS)
         for a in range(K_BLOCKS):
             nc.scalar.dma_start(windows[a][:], table_rows[:, a, :])
@@ -45,7 +46,7 @@ def tile_gather_matmul_kernel(tc, table, w, b, offs, out):
                 )
 
         z = held.tile([P, N], F32, name="z")
-        pooled = held.tile([P, N // NEIGHBOURS], F32, name="pooled")
+        pooled = held.tile([P, N // NEIGHBOURS], F32, name="pooled", align_bytes=ROW_ALIGN)
         for i in range(PIECES):
             z_piece = z[:, i * PIECE : (i + 1) * PIECE]
             nc.scalar.activation(z_piece, y[i][:], mybir.ActivationFunctionType.Gelu_apprx_tanh, bias=bias[:, 0:1])

@@ -9,6 +9,8 @@ NEIGHBOURS = 4
 PIECES = 2
 PIECE = N // PIECES
 ROW_ALIGN = 256
+SLICES = 2
+SLICE = PIECE // SLICES
 FLOPS = 2 * K * M * N
 
 
@@ -48,12 +50,19 @@ def tile_gather_matmul_kernel(tc, table, w, b, offs, out):
         z = held.tile([P, N], F32, name="z")
         pooled = held.tile([P, N // NEIGHBOURS], F32, name="pooled", align_bytes=ROW_ALIGN)
         for i in range(PIECES):
-            z_piece = z[:, i * PIECE : (i + 1) * PIECE]
-            nc.scalar.activation(z_piece, y[i][:], mybir.ActivationFunctionType.Gelu_apprx_tanh, bias=bias[:, 0:1])
-            nc.vector.tensor_reduce(
-                pooled[:, i * (PIECE // NEIGHBOURS) : (i + 1) * (PIECE // NEIGHBOURS)],
-                z_piece.rearrange("p (v t) -> p v t", t=NEIGHBOURS),
-                axis=mybir.AxisListType.X,
-                op=mybir.AluOpType.max,
-            )
+            for s in range(SLICES):
+                first = i * PIECE + s * SLICE
+                z_slice = z[:, first : first + SLICE]
+                nc.scalar.activation(
+                    z_slice,
+                    y[i][:, s * SLICE : (s + 1) * SLICE],
+                    mybir.ActivationFunctionType.Gelu_apprx_tanh,
+                    bias=bias[:, 0:1],
+                )
+                nc.vector.tensor_reduce(
+                    pooled[:, first // NEIGHBOURS : (first + SLICE) // NEIGHBOURS],
+                    z_slice.rearrange("p (v t) -> p v t", t=NEIGHBOURS),
+                    axis=mybir.AxisListType.X,
+                    op=mybir.AluOpType.max,
+                )
         nc.sync.dma_start(out, pooled[:])

@@ -9,6 +9,7 @@ NEIGHBOURS = 4
 PIECES = 2
 PIECE = N // PIECES
 ROW_ALIGN = 256
+OUT_PIECE = PIECE // NEIGHBOURS
 SLICES = 2
 SLICE = PIECE // SLICES
 FLOPS = 2 * K * M * N
@@ -24,12 +25,12 @@ def tile_gather_matmul_kernel(tc, table, w, b, offs, out):
         nc.sync.dma_start(offsets[:], offs)
         weights = held.tile([P, K_BLOCKS, M], BF16, name="weights", align_bytes=ROW_ALIGN)
         nc.sync.dma_start(weights[:], w.rearrange("(p a) m -> p a m", a=K_BLOCKS))
-        bias = held.tile([P, 1], F32, name="bias", align_bytes=ROW_ALIGN)
-        nc.sync.dma_start(bias[:], b)
         windows = [held.tile([P, S], BF16, name="window%d" % a, align_bytes=ROW_ALIGN) for a in range(K_BLOCKS)]
         table_rows = table.rearrange("(p a) s -> p a s", a=K_BLOCKS)
         for a in range(K_BLOCKS):
             nc.scalar.dma_start(windows[a][:], table_rows[:, a, :])
+        bias = held.tile([P, 1], F32, name="bias", align_bytes=ROW_ALIGN)
+        nc.scalar.dma_start(bias[:], b)
 
         warm_in = held.tile([P, 1], F32, name="warm_in")
         warm_out = held.tile([P, 1], F32, name="warm_out")
@@ -48,8 +49,8 @@ def tile_gather_matmul_kernel(tc, table, w, b, offs, out):
                 )
 
         z = held.tile([P, N], F32, name="z")
-        pooled = held.tile([P, N // NEIGHBOURS], F32, name="pooled", align_bytes=ROW_ALIGN)
         for i in range(PIECES):
+            pooled = held.tile([P, OUT_PIECE], F32, name="pooled%d" % i, align_bytes=ROW_ALIGN)
             for s in range(SLICES):
                 first = i * PIECE + s * SLICE
                 z_slice = z[:, first : first + SLICE]
@@ -60,9 +61,9 @@ def tile_gather_matmul_kernel(tc, table, w, b, offs, out):
                     bias=bias[:, 0:1],
                 )
                 nc.vector.tensor_reduce(
-                    pooled[:, first // NEIGHBOURS : (first + SLICE) // NEIGHBOURS],
+                    pooled[:, s * (SLICE // NEIGHBOURS) : (s + 1) * (SLICE // NEIGHBOURS)],
                     z_slice.rearrange("p (v t) -> p v t", t=NEIGHBOURS),
                     axis=mybir.AxisListType.X,
                     op=mybir.AluOpType.max,
                 )
-        nc.sync.dma_start(out, pooled[:])
+            nc.sync.dma_start(out[:, i * OUT_PIECE : (i + 1) * OUT_PIECE], pooled[:])

import concourse.mybir as mybir

BF16, F32, U16 = mybir.dt.bfloat16, mybir.dt.float32, mybir.dt.uint16

P = 128
K, S, M, N = 256, 1024, 128, 256
K_BLOCKS = K // P
NEIGHBOURS = 4
PIECES = 2
PIECE = N // PIECES
ROW_ALIGN = 256
OUT_PIECE = PIECE // NEIGHBOURS
SLICES = 2
SLICE = PIECE // SLICES
FLOPS = 2 * K * M * N


def tile_gather_matmul_kernel(tc, table, w, b, offs, out):
    nc = tc.nc
    with (
        tc.tile_pool(name="held", bufs=1) as held,
        tc.psum_pool(name="psum", bufs=1) as psum,
    ):
        offsets = held.tile([P, N // 16], U16, name="offsets", align_bytes=ROW_ALIGN)
        nc.sync.dma_start(offsets[:], offs)
        weights = held.tile([P, K_BLOCKS, M], BF16, name="weights", align_bytes=ROW_ALIGN)
        nc.sync.dma_start(weights[:], w.rearrange("(p a) m -> p a m", a=K_BLOCKS))
        windows = [held.tile([P, S], BF16, name="window%d" % a, align_bytes=ROW_ALIGN) for a in range(K_BLOCKS)]
        table_rows = table.rearrange("(p a) s -> p a s", a=K_BLOCKS)
        for a in range(K_BLOCKS):
            nc.scalar.dma_start(windows[a][:], table_rows[:, a, :])
        bias = held.tile([P, 1], F32, name="bias", align_bytes=ROW_ALIGN)
        nc.scalar.dma_start(bias[:], b)

        warm_in = held.tile([P, 1], F32, name="warm_in")
        warm_out = held.tile([P, 1], F32, name="warm_out")
        nc.vector.memset(warm_in[:], 0.0)
        nc.scalar.activation(warm_out[:], warm_in[:], mybir.ActivationFunctionType.Gelu_apprx_tanh)

        y = [psum.tile([P, PIECE], F32, name="y%d" % i) for i in range(PIECES)]
        for a in range(K_BLOCKS):
            for i in range(PIECES):
                nc.tensor.matmul(
                    y[i][:],
                    weights[:, a, :],
                    windows[a][:].indirect(offsets[:, i * (PIECE // 16) : (i + 1) * (PIECE // 16)]),
                    start=(a == 0),
                    stop=(a == K_BLOCKS - 1),
                )

        z = held.tile([P, N], F32, name="z")
        for i in range(PIECES):
            pooled = held.tile([P, OUT_PIECE], F32, name="pooled%d" % i, align_bytes=ROW_ALIGN)
            for s in range(SLICES):
                first = i * PIECE + s * SLICE
                z_slice = z[:, first : first + SLICE]
                nc.scalar.activation(
                    z_slice,
                    y[i][:, s * SLICE : (s + 1) * SLICE],
                    mybir.ActivationFunctionType.Gelu_apprx_tanh,
                    bias=bias[:, 0:1],
                )
                nc.vector.tensor_reduce(
                    pooled[:, s * (SLICE // NEIGHBOURS) : (s + 1) * (SLICE // NEIGHBOURS)],
                    z_slice.rearrange("p (v t) -> p v t", t=NEIGHBOURS),
                    axis=mybir.AxisListType.X,
                    op=mybir.AluOpType.max,
                )
            nc.sync.dma_start(out[:, i * OUT_PIECE : (i + 1) * OUT_PIECE], pooled[:])
